import numpy as np
import ml_dtypes


def mxq(x, axis, fmt="e4m3"):
    dtype, down = {"e4m3": (ml_dtypes.float8_e4m3fn, 7), "e5m2": (ml_dtypes.float8_e5m2, 14)}[fmt]
    v = np.moveaxis(np.asarray(x, np.float32).astype(ml_dtypes.bfloat16).astype(np.float64), axis, -1)
    blocks = v.reshape(v.shape[:-1] + (-1, 32))
    amax = np.abs(blocks).max(-1, keepdims=True)
    byte = np.maximum(np.where(amax > 0, np.frexp(amax)[1] - 1 + 127, 0) - down, 1)
    scale = np.exp2(byte - 127.0)
    codes = (blocks / scale).astype(np.float32).astype(dtype).astype(np.float64)
    return np.moveaxis((codes * scale).reshape(v.shape), -1, axis)


WIDE = False


def mx_kscale(k):
    if not WIDE:
        return np.ones(k)
    levels = np.array([10, -10, 5, -5, 0])
    if k % 512:
        return np.exp2(np.random.permutation(np.resize(levels, k // 32))).repeat(32)
    a = np.empty((k // 512, 16))
    for p in range(k // 512):
        a[p, :8] = np.random.permutation(np.resize(levels, 8))
        for g in range(8):
            far = levels[np.abs(levels - a[p, g]) >= 10]
            a[p, g + 8] = far[np.random.randint(len(far))]
    return np.exp2(a.ravel()).repeat(32)


def f64(x):
    return np.asarray(x).astype(np.float64)


def striped(idx):
    return np.tile(idx.reshape(-1, 16).T, (8, 1)).astype(np.uint16)


def unstriped(offs):
    return offs[:16].T.reshape(-1).astype(np.int64)


def striped8(idx):
    return np.concatenate([x.reshape(-1, 16).T for x in idx]).astype(np.uint16)


def runs(offs, k):
    lists = np.stack([offs[16 * r : 16 * r + 16].T.reshape(-1) for r in range(8)]).astype(np.int64)
    return lists[np.arange(k) % 512 // 64]


def pack_weight(w):
    k, n = w.shape
    w = f64(np.asarray(w, np.float32).astype(ml_dtypes.bfloat16)).reshape(k // 32, 32, n)
    amax = np.abs(w).max(1)
    byte = np.clip(np.where(amax > 0, np.frexp(amax)[1] - 1 + 127 - 7, 1), 1, 254)
    scaled = (w * np.exp2(127.0 - byte)[:, None, :]).reshape(k, n).astype(np.float32)
    words = np.ascontiguousarray(scaled.reshape(k // 512, 128, 4, n).transpose(0, 1, 3, 2)).astype(ml_dtypes.float8_e4m3fn).view(np.uint8)
    return words, np.ascontiguousarray(byte.astype(np.uint8).reshape(k // 512, 16, n))


def unpack_weight(words, scales):
    g, p, n, _ = words.shape
    vals = np.ascontiguousarray(words).view(ml_dtypes.float8_e4m3fn).astype(np.float64) * np.repeat(np.exp2(scales.astype(np.float64) - 127.0), 8, axis=1)[..., None]
    return vals.transpose(0, 1, 3, 2).reshape(g * 512, n)


K, T, S, V, N, H, W, U = 512, 2048, 512, 512, 512, 512, 256, 1024


def setup_inputs():
    n = np.random.standard_normal
    s = mx_kscale(K)[:, None]
    u = mx_kscale(S)
    packed_xT = pack_weight(n((K, T)) * s)
    perm = np.stack([np.random.permutation(S) for _ in range(8)])
    return {
        "x_words": packed_xT[0],
        "x_scales": packed_xT[1],
        "w1": (n((K, H)) / np.sqrt(K) / s).astype(np.float32),
        "w2": (n((K, H)) / np.sqrt(K) / s).astype(np.float32),
        "ga": (np.random.uniform(0.5, 1.5, (H, 1)) * u[:, None]).astype(np.float32),
        "gb": (np.random.uniform(0.5, 1.5, (H, 1)) / u[:, None]).astype(np.float32),
        "mem": n((S, U)).astype(np.float32),
        "gt": (np.random.uniform(0.5, 1.5, (S, 1)) * u[:, None]).astype(np.float32),
        "res": (1.5 * n((N, U))).astype(np.float32),
        "w3": (n((S, N)) / np.sqrt(S) / u[:, None]).astype(np.float32),
        "offs": striped(np.random.permutation(T)[:S]),
        "two": striped(np.random.permutation(T)[:V]),
        "n1": striped8(perm[:, :W]),
        "n2": striped8(perm[:, W:]),
        "n3": striped8(np.stack([np.random.permutation(U)[:V] for _ in range(8)])),
    }


def reference(x_words, x_scales, w1, w2, ga, gb, mem, gt, res, w3, offs, two, n1, n2, n3):
    xq = unpack_weight(x_words, x_scales)[:, unstriped(offs)]
    a = mxq(f64(w1), 0, "e4m3").T @ xq
    pa = a[np.arange(H)[:, None], runs(n1, H)]
    pb = a[np.arange(H)[:, None], runs(n2, H)]
    rb = np.maximum(0.5 * pa, pb)
    ra = pb - pa
    ds = np.zeros((H, S))
    ds[np.arange(H)[:, None], runs(n1, H)] = ra
    dt = ds.copy()
    dt[np.arange(H)[:, None], runs(n2, H)] = rb
    z = f64(ga) * dt
    x_two = unpack_weight(x_words, x_scales)[:, unstriped(two)]
    b = mxq(f64(w2), 0, "e4m3").T @ x_two
    z2 = f64(gb) * b
    s = 0.0625 * ((mxq(z, 0, "e4m3").T @ mxq(z2, 0, "e4m3")))
    nw = np.maximum(s, 0.5 * (f64(mem)[np.arange(S)[:, None], runs(n3, S)]))
    pg = f64(mem).copy()
    pg[np.arange(S)[:, None], runs(n3, S)] = nw
    z3 = f64(gt) * pg
    return f64(res) + (mxq(f64(w3), 0, "e4m3").T @ mxq(z3, 0, "e4m3"))

@@ -1,0 +1,207 @@
+from contextlib import ExitStack
+
+import concourse.mybir as mybir
+
+K, T, S, V, N, H, W, U = 512, 2048, 512, 512, 512, 512, 256, 1024
+FLOPS = 2 * 512 * 512 * 512 * 3 + 2 * 512 * 512 * 1024
+
+F32 = mybir.dt.float32
+BF16 = mybir.dt.bfloat16
+I32 = mybir.dt.int32
+U32 = mybir.dt.uint32
+U16 = mybir.dt.uint16
+U8 = mybir.dt.uint8
+FP8X4 = mybir.dt.float8_e4m3fn_x4
+MULT = mybir.AluOpType.mult
+ADD = mybir.AluOpType.add
+MAX = mybir.AluOpType.max
+COPY = mybir.ActivationFunctionType.Copy
+
+P = 128
+PACK = 4
+OUT_CHUNK = 256
+
+
+def tile_picked_valliftpagex_none_p_kernel(
+    tc, x_words, x_scales, w1, w2, ga, gb, mem, gt, res, w3, offs, two, n1, n2, n3, out
+):
+    nc = tc.nc
+    with ExitStack() as ctx:
+        lists = ctx.enter_context(tc.tile_pool(name="lists", bufs=1))
+        sb = ctx.enter_context(tc.tile_pool(name="sb", bufs=1))
+        psum = ctx.enter_context(tc.psum_pool(name="psum", bufs=1))
+
+        def load_list(src, name):
+            tile = lists.tile(list(src.shape), U16, name=name)
+            nc.sync.dma_start(tile[:], src)
+            return tile
+
+        def mx_tiles(name, width):
+            codes = sb.tile([P, width], U32, name=name + "_codes", align_bytes=64)
+            scales = sb.tile([P, width], U8, name=name + "_scales", align_bytes=64)
+            return codes, scales
+
+        def quantize(name, grouped, width):
+            codes, scales = mx_tiles(name, width)
+            nc.vector.quantize_mx(out=codes[:].bitcast(FP8X4), scales=scales[:], in_=grouped)
+            return codes, scales
+
+        def product(acc, stationary, cols, moving):
+            nc.tensor.matmul_mx(
+                out=acc,
+                lhsT=stationary[0][:, cols].bitcast(FP8X4),
+                lhsT_scale=stationary[1][:, cols],
+                rhs=moving[0][:].bitcast(FP8X4),
+                rhs_scale=moving[1][:],
+                start=True,
+                stop=True,
+            )
+
+        def bank(number, shape):
+            return psum.tile(shape, F32, name="bank%d" % number, tag="bank%d" % number)
+
+        offs_sb = load_list(offs, "offs_sb")
+        two_sb = load_list(two, "two_sb")
+        xs_all = sb.tile([P, T], U8, name="xs_all", align_bytes=64)
+        nc.vector.memset(xs_all[:].bitcast(I32), 0)
+        for q in range(4):
+            nc.sync.dma_start(xs_all[32 * q : 32 * q + 4, :].bitcast(I32), x_scales[0, 4 * q : 4 * q + 4, :].bitcast(I32))
+        w1_rows = w1.rearrange("(p j) c -> p j c", j=PACK)
+        w1_raw = []
+        for half in range(2):
+            tile = sb.tile([P, PACK, H // 2], F32, name="w1_raw%d" % half)
+            nc.sync.dma_start(tile[:], w1_rows[:, :, half * (H // 2) : (half + 1) * (H // 2)])
+            w1_raw.append(tile)
+        xw_all = sb.tile([P, T], U32, name="xw_all", align_bytes=64)
+        nc.sync.dma_start(xw_all[:].bitcast(I32), x_words[0].rearrange("p n t -> p (n t)").bitcast(I32))
+        n1_sb = load_list(n1, "n1_sb")
+        n2_sb = load_list(n2, "n2_sb")
+        w2_raw = sb.tile([P, PACK, H], F32, name="w2_raw")
+        nc.sync.dma_start(w2_raw[:], w2.rearrange("(p j) c -> p j c", j=PACK))
+        w3_raw = sb.tile([P, PACK, N], F32, name="w3_raw")
+        nc.sync.dma_start(w3_raw[:], w3.rearrange("(p j) c -> p j c", j=PACK))
+        gains = []
+        for name, src in (("ga_sb", ga), ("gb_sb", gb), ("gt_sb", gt)):
+            tile = sb.tile([P, PACK], F32, name=name)
+            nc.sync.dma_start(tile[:], src.rearrange("(p t) o -> p (t o)", t=PACK))
+            gains.append(tile)
+        ga_sb, gb_sb, gt_sb = gains
+        n3_sb = load_list(n3, "n3_sb")
+        mem_rows = mem.rearrange("(p t) w -> t p w", t=PACK)
+        page = []
+        for t in range(PACK):
+            tile = sb.tile([P, U], F32, name="page%d" % t)
+            nc.sync.dma_start(tile[:], mem_rows[t])
+            page.append(tile)
+        res_rows = res.rearrange("(mt p) w -> p mt w", p=P)
+        out_rows = out.rearrange("(mt p) w -> p mt w", p=P)
+        res_sb = {}
+        for c in range(U // OUT_CHUNK):
+            for pair in range(2):
+                tile = sb.tile([P, 2, OUT_CHUNK], F32, name="res%d_%d" % (c, pair))
+                nc.sync.dma_start(tile[:], res_rows[:, 2 * pair : 2 * pair + 2, c * OUT_CHUNK : (c + 1) * OUT_CHUNK])
+                res_sb[c, pair] = tile
+
+        xa = mx_tiles("xa", S)
+        xb = mx_tiles("xb", V)
+        nc.vector.tensor_copy(xa[1][:], xs_all[:].indirect(offs_sb[:]))
+        nc.vector.tensor_copy(xb[1][:], xs_all[:].indirect(two_sb[:]))
+
+        w1_bf = sb.tile([P, PACK, P, PACK], BF16, name="w1_bf", align_bytes=64)
+        for half in range(2):
+            nc.scalar.copy(
+                w1_bf[:, :, half * 64 : (half + 1) * 64, :].rearrange("p t m j -> p m t j"),
+                w1_raw[half][:].rearrange("p j (m t) -> p m t j", t=PACK),
+            )
+        w1_q = quantize("w1", w1_bf[:].rearrange("p t m j -> p (t m j)"), H)
+        nc.vector.tensor_copy(xa[0][:], xw_all[:].indirect(offs_sb[:]))
+        nc.vector.tensor_copy(xb[0][:], xw_all[:].indirect(two_sb[:]))
+
+        a_sb = []
+        for t in range(PACK):
+            acc = bank(t, [P, S])
+            product(acc[:], w1_q, slice(t * P, (t + 1) * P), xa)
+            tile = sb.tile([P, S], F32, name="a%d" % t)
+            nc.scalar.copy(tile[:], acc[:])
+            a_sb.append(tile)
+
+        w2_bf = sb.tile([P, PACK, P, PACK], BF16, name="w2_bf", tag="w2_bf_then_rb", align_bytes=64)
+        nc.scalar.copy(w2_bf[:].rearrange("p t m j -> p m t j"), w2_raw[:].rearrange("p j (m t) -> p m t j", t=PACK))
+        w3_bf = sb.tile([P, N, PACK], BF16, name="w3_bf", align_bytes=64)
+        nc.scalar.copy(
+            w3_bf[:].rearrange("p (c i) j -> p c j i", i=4), w3_raw[:].rearrange("p j (c i) -> p c j i", i=4)
+        )
+
+        neg_pa = sb.tile([P, PACK, W], F32, name="neg_pa")
+        pb = sb.tile([P, PACK, W], F32, name="pb")
+        for t in range(PACK):
+            nc.vector.tensor_scalar(neg_pa[:, t, :], a_sb[t][:].indirect(n1_sb[:]), -1.0, 0.0, MULT, ADD)
+            nc.vector.tensor_copy(pb[:, t, :], a_sb[t][:].indirect(n2_sb[:]))
+
+        w2_q = quantize("w2", w2_bf[:].rearrange("p t m j -> p (t m j)"), H)
+        z2_rows = sb.tile([P, PACK, V], BF16, name="z2_rows", tag="z2_rows_then_ga")
+        for t in range(PACK):
+            acc = bank(PACK + t, [P, V])
+            product(acc[:], w2_q, slice(t * P, (t + 1) * P), xb)
+            nc.scalar.activation(z2_rows[:, t, :], acc[:], COPY, scale=gb_sb[:, t : t + 1])
+        z2_bf = sb.tile([P, V, PACK], BF16, name="z2_bf", align_bytes=64)
+        nc.scalar.copy(
+            z2_bf[:].rearrange("p (c i) t -> p c t i", i=4), z2_rows[:].rearrange("p t (c i) -> p c t i", i=4)
+        )
+        ga_late = sb.tile([P, PACK], F32, name="ga_late", tag="z2_rows_then_ga")
+        nc.scalar.copy(ga_late[:], ga_sb[:])
+
+        rb = sb.tile([P, PACK, W], F32, name="rb", tag="w2_bf_then_rb", align_bytes=64)
+        nc.vector.scalar_tensor_tensor(
+            rb[:].rearrange("p t w -> p (t w)"),
+            neg_pa[:].rearrange("p t w -> p (t w)"),
+            -0.5,
+            pb[:].rearrange("p t w -> p (t w)"),
+            MULT,
+            MAX,
+        )
+        dt = [sb.tile([P, S], F32, name="dt%d" % t) for t in range(PACK)]
+        z_bf = [sb.tile([P, P, PACK], BF16, name="z_bf%d" % r, align_bytes=64) for r in range(PACK)]
+        for pair in range(2):
+            for t in (2 * pair, 2 * pair + 1):
+                nc.vector.tensor_copy(dt[t][:].indirect(n2_sb[:]), rb[:, t, :])
+            for t in (2 * pair, 2 * pair + 1):
+                nc.vector.tensor_tensor(dt[t][:].indirect(n1_sb[:]), pb[:, t, :], neg_pa[:, t, :], ADD)
+            for t in (2 * pair, 2 * pair + 1):
+                for r in range(PACK):
+                    nc.scalar.activation(z_bf[r][:, :, t], dt[t][:, r::PACK], COPY, scale=ga_late[:, t : t + 1])
+
+        w3_q = quantize("w3", w3_bf[:].rearrange("p c j -> p (c j)"), N)
+        z2_q = quantize("z2", z2_bf[:].rearrange("p c t -> p (c t)"), V)
+        half_old = sb.tile([P, PACK, V], F32, name="half_old")
+        for t in range(PACK):
+            nc.vector.tensor_scalar(half_old[:, t, :], page[t][:].indirect(n3_sb[:]), 0.5, 0.0, MULT, ADD)
+
+        s_acc = []
+        for r in range(PACK):
+            z_q = quantize("z_cols%d" % r, z_bf[r][:].rearrange("p m t -> p (m t)"), P)
+            acc = bank(r, [P, V])
+            product(acc[:], z_q, slice(0, P), z2_q)
+            s_acc.append(acc)
+
+        z3_bf = [sb.tile([P, OUT_CHUNK, PACK], BF16, name="z3_bf%d" % c, align_bytes=64) for c in range(U // OUT_CHUNK)]
+        nw = sb.tile([P, PACK, V], F32, name="nw")
+        for t in range(PACK):
+            nc.vector.scalar_tensor_tensor(nw[:, t, :], s_acc[t][:], 0.0625, half_old[:, t, :], MULT, MAX)
+        for t in range(PACK):
+            nc.vector.tensor_copy(page[t][:].indirect(n3_sb[:]), nw[:, t, :])
+            for c in range(U // OUT_CHUNK):
+                nc.scalar.activation(
+                    z3_bf[c][:, :, t], page[t][:, c * OUT_CHUNK : (c + 1) * OUT_CHUNK], COPY, scale=gt_sb[:, t : t + 1]
+                )
+
+        for c in range(U // OUT_CHUNK):
+            z3_q = quantize("z3_%d" % c, z3_bf[c][:].rearrange("p w t -> p (w t)"), OUT_CHUNK)
+            for pair in range(2):
+                acc = bank((PACK + 2 * c + pair) % 8, [P, 2, OUT_CHUNK])
+                for i in range(2):
+                    mt = 2 * pair + i
+                    product(acc[:, i, :], w3_q, slice(mt * P, (mt + 1) * P), z3_q)
+                result = sb.tile([P, 2, OUT_CHUNK], F32, name="result%d_%d" % (c, pair))
+                nc.vector.tensor_tensor(result[:], acc[:], res_sb[c, pair][:], ADD)
+                nc.sync.dma_start(out_rows[:, 2 * pair : 2 * pair + 2, c * OUT_CHUNK : (c + 1) * OUT_CHUNK], result[:])

@@ -19,7 +19,9 @@ COPY = mybir.ActivationFunctionType.Copy
 
 P = 128
 PACK = 4
-OUT_CHUNK = 256
+OUT_CHUNKS = (128, 128, 256, 256, 256)
+BANK = 512
+W1_PARTS = 4
 
 
 def tile_picked_valliftpagex_none_p_kernel(
@@ -36,13 +38,13 @@ def tile_picked_valliftpagex_none_p_kernel(
             nc.sync.dma_start(tile[:], src)
             return tile
 
-        def mx_tiles(name, width):
-            codes = sb.tile([P, width], U32, name=name + "_codes", align_bytes=64)
+        def mx_tiles(name, width, tag=None):
+            codes = sb.tile([P, width], U32, name=name + "_codes", tag=tag or name + "_codes", align_bytes=64)
             scales = sb.tile([P, width], U8, name=name + "_scales", align_bytes=64)
             return codes, scales
 
-        def quantize(name, grouped, width):
-            codes, scales = mx_tiles(name, width)
+        def quantize(name, grouped, width, tag=None):
+            codes, scales = mx_tiles(name, width, tag)
             nc.vector.quantize_mx(out=codes[:].bitcast(FP8X4), scales=scales[:], in_=grouped)
             return codes, scales
 
@@ -62,45 +64,54 @@ def tile_picked_valliftpagex_none_p_kernel(
 
         offs_sb = load_list(offs, "offs_sb")
         two_sb = load_list(two, "two_sb")
+        w1_rows = w1.rearrange("(p j) c -> p j c", j=PACK)
+        w1_raw = [sb.tile([P, PACK, H // W1_PARTS], F32, name="w1_raw%d" % part) for part in range(W1_PARTS)]
+
+        def load_w1(part):
+            nc.sync.dma_start(w1_raw[part][:], w1_rows[:, :, part * (H // W1_PARTS) : (part + 1) * (H // W1_PARTS)])
+
+        load_w1(0)
         xs_all = sb.tile([P, T], U8, name="xs_all", align_bytes=64)
         nc.vector.memset(xs_all[:].bitcast(I32), 0)
         for q in range(4):
             nc.sync.dma_start(xs_all[32 * q : 32 * q + 4, :].bitcast(I32), x_scales[0, 4 * q : 4 * q + 4, :].bitcast(I32))
-        w1_rows = w1.rearrange("(p j) c -> p j c", j=PACK)
-        w1_raw = []
-        for half in range(2):
-            tile = sb.tile([P, PACK, H // 2], F32, name="w1_raw%d" % half)
-            nc.sync.dma_start(tile[:], w1_rows[:, :, half * (H // 2) : (half + 1) * (H // 2)])
-            w1_raw.append(tile)
+        for part in range(1, W1_PARTS):
+            load_w1(part)
         xw_all = sb.tile([P, T], U32, name="xw_all", align_bytes=64)
         nc.sync.dma_start(xw_all[:].bitcast(I32), x_words[0].rearrange("p n t -> p (n t)").bitcast(I32))
+        n3_sb = load_list(n3, "n3_sb")
+        mem_rows = mem.rearrange("(p t) w -> t p w", t=PACK)
+        page = [sb.tile([P, U], F32, name="page%d" % t) for t in range(PACK)]
+        nc.sync.dma_start(page[0][:], mem_rows[0])
         n1_sb = load_list(n1, "n1_sb")
         n2_sb = load_list(n2, "n2_sb")
         w2_raw = sb.tile([P, PACK, H], F32, name="w2_raw")
         nc.sync.dma_start(w2_raw[:], w2.rearrange("(p j) c -> p j c", j=PACK))
-        w3_raw = sb.tile([P, PACK, N], F32, name="w3_raw")
-        nc.sync.dma_start(w3_raw[:], w3.rearrange("(p j) c -> p j c", j=PACK))
         gains = []
-        for name, src in (("ga_sb", ga), ("gb_sb", gb), ("gt_sb", gt)):
+        for name, src in (("gb_sb", gb), ("ga_sb", ga), ("gt_sb", gt)):
             tile = sb.tile([P, PACK], F32, name=name)
             nc.sync.dma_start(tile[:], src.rearrange("(p t) o -> p (t o)", t=PACK))
             gains.append(tile)
-        ga_sb, gb_sb, gt_sb = gains
-        n3_sb = load_list(n3, "n3_sb")
-        mem_rows = mem.rearrange("(p t) w -> t p w", t=PACK)
-        page = []
-        for t in range(PACK):
-            tile = sb.tile([P, U], F32, name="page%d" % t)
-            nc.sync.dma_start(tile[:], mem_rows[t])
-            page.append(tile)
+        gb_sb, ga_sb, gt_sb = gains
+        for t in range(1, PACK):
+            nc.sync.dma_start(page[t][:], mem_rows[t])
+        w3_raw = sb.tile([P, PACK, N], F32, name="w3_raw")
+        nc.sync.dma_start(w3_raw[:], w3.rearrange("(p j) c -> p j c", j=PACK))
         res_rows = res.rearrange("(mt p) w -> p mt w", p=P)
         out_rows = out.rearrange("(mt p) w -> p mt w", p=P)
-        res_sb = {}
-        for c in range(U // OUT_CHUNK):
-            for pair in range(2):
-                tile = sb.tile([P, 2, OUT_CHUNK], F32, name="res%d_%d" % (c, pair))
-                nc.sync.dma_start(tile[:], res_rows[:, 2 * pair : 2 * pair + 2, c * OUT_CHUNK : (c + 1) * OUT_CHUNK])
-                res_sb[c, pair] = tile
+        chunks = []
+        start = 0
+        for width in OUT_CHUNKS:
+            chunks.append(slice(start, start + width))
+            start = start + width
+        pieces = []
+        for c, cols in enumerate(chunks):
+            per_bank = BANK // OUT_CHUNKS[c]
+            for first in range(0, PACK, per_bank):
+                rows = slice(first, first + per_bank)
+                tile = sb.tile([P, per_bank, OUT_CHUNKS[c]], F32, name="res%d_%d" % (c, first))
+                nc.sync.dma_start(tile[:], res_rows[:, rows, cols])
+                pieces.append((c, rows, tile))
 
         xa = mx_tiles("xa", S)
         xb = mx_tiles("xb", V)
@@ -108,14 +119,23 @@ def tile_picked_valliftpagex_none_p_kernel(
         nc.vector.tensor_copy(xb[1][:], xs_all[:].indirect(two_sb[:]))
 
         w1_bf = sb.tile([P, PACK, P, PACK], BF16, name="w1_bf", align_bytes=64)
-        for half in range(2):
-            nc.scalar.copy(
-                w1_bf[:, :, half * 64 : (half + 1) * 64, :].rearrange("p t m j -> p m t j"),
-                w1_raw[half][:].rearrange("p j (m t) -> p m t j", t=PACK),
+        part_m = P // W1_PARTS
+        for part in range(W1_PARTS):
+            cast = nc.vector.tensor_copy if part == W1_PARTS - 1 else nc.scalar.copy
+            cast(
+                w1_bf[:, :, part * part_m : (part + 1) * part_m, :].rearrange("p t m j -> p m t j"),
+                w1_raw[part][:].rearrange("p j (m t) -> p m t j", t=PACK),
             )
         w1_q = quantize("w1", w1_bf[:].rearrange("p t m j -> p (t m j)"), H)
         nc.vector.tensor_copy(xa[0][:], xw_all[:].indirect(offs_sb[:]))
         nc.vector.tensor_copy(xb[0][:], xw_all[:].indirect(two_sb[:]))
+
+        def gather_half_old(t, tag):
+            tile = sb.tile([P, V], F32, name="half_old%d" % t, tag=tag, align_bytes=64)
+            nc.vector.tensor_scalar(tile[:], page[t][:].indirect(n3_sb[:]), 0.5, 0.0, MULT, ADD)
+            return tile
+
+        half_old = [gather_half_old(0, "half_old0")]
 
         a_sb = []
         for t in range(PACK):
@@ -127,19 +147,16 @@ def tile_picked_valliftpagex_none_p_kernel(
 
         w2_bf = sb.tile([P, PACK, P, PACK], BF16, name="w2_bf", tag="w2_bf_then_rb", align_bytes=64)
         nc.scalar.copy(w2_bf[:].rearrange("p t m j -> p m t j"), w2_raw[:].rearrange("p j (m t) -> p m t j", t=PACK))
-        w3_bf = sb.tile([P, N, PACK], BF16, name="w3_bf", align_bytes=64)
-        nc.scalar.copy(
-            w3_bf[:].rearrange("p (c i) j -> p c j i", i=4), w3_raw[:].rearrange("p j (c i) -> p c j i", i=4)
-        )
 
-        neg_pa = sb.tile([P, PACK, W], F32, name="neg_pa")
+        neg_pa = sb.tile([P, PACK, W], F32, name="neg_pa", tag="neg_pa_then_half_old2", align_bytes=64)
         pb = sb.tile([P, PACK, W], F32, name="pb")
         for t in range(PACK):
             nc.vector.tensor_scalar(neg_pa[:, t, :], a_sb[t][:].indirect(n1_sb[:]), -1.0, 0.0, MULT, ADD)
             nc.vector.tensor_copy(pb[:, t, :], a_sb[t][:].indirect(n2_sb[:]))
 
+        half_old.append(gather_half_old(1, "half_old1"))
         w2_q = quantize("w2", w2_bf[:].rearrange("p t m j -> p (t m j)"), H)
-        z2_rows = sb.tile([P, PACK, V], BF16, name="z2_rows", tag="z2_rows_then_ga")
+        z2_rows = sb.tile([P, PACK, V], BF16, name="z2_rows", tag="z2_rows_then_ga", align_bytes=64)
         for t in range(PACK):
             acc = bank(PACK + t, [P, V])
             product(acc[:], w2_q, slice(t * P, (t + 1) * P), xb)
@@ -148,7 +165,7 @@ def tile_picked_valliftpagex_none_p_kernel(
         nc.scalar.copy(
             z2_bf[:].rearrange("p (c i) t -> p c t i", i=4), z2_rows[:].rearrange("p t (c i) -> p c t i", i=4)
         )
-        ga_late = sb.tile([P, PACK], F32, name="ga_late", tag="z2_rows_then_ga")
+        ga_late = sb.tile([P, PACK], F32, name="ga_late", tag="z2_rows_then_ga", align_bytes=64)
         nc.scalar.copy(ga_late[:], ga_sb[:])
 
         rb = sb.tile([P, PACK, W], F32, name="rb", tag="w2_bf_then_rb", align_bytes=64)
@@ -162,20 +179,24 @@ def tile_picked_valliftpagex_none_p_kernel(
         )
         dt = [sb.tile([P, S], F32, name="dt%d" % t) for t in range(PACK)]
         z_bf = [sb.tile([P, P, PACK], BF16, name="z_bf%d" % r, align_bytes=64) for r in range(PACK)]
-        for pair in range(2):
-            for t in (2 * pair, 2 * pair + 1):
-                nc.vector.tensor_copy(dt[t][:].indirect(n2_sb[:]), rb[:, t, :])
-            for t in (2 * pair, 2 * pair + 1):
-                nc.vector.tensor_tensor(dt[t][:].indirect(n1_sb[:]), pb[:, t, :], neg_pa[:, t, :], ADD)
-            for t in (2 * pair, 2 * pair + 1):
-                for r in range(PACK):
-                    nc.scalar.activation(z_bf[r][:, :, t], dt[t][:, r::PACK], COPY, scale=ga_late[:, t : t + 1])
 
-        w3_q = quantize("w3", w3_bf[:].rearrange("p c j -> p (c j)"), N)
-        z2_q = quantize("z2", z2_bf[:].rearrange("p c t -> p (c t)"), V)
-        half_old = sb.tile([P, PACK, V], F32, name="half_old")
+        def put_rb(t):
+            nc.vector.tensor_copy(dt[t][:].indirect(n2_sb[:]), rb[:, t, :])
+
+        put_rb(0)
         for t in range(PACK):
-            nc.vector.tensor_scalar(half_old[:, t, :], page[t][:].indirect(n3_sb[:]), 0.5, 0.0, MULT, ADD)
+            if t + 1 < PACK:
+                put_rb(t + 1)
+            nc.vector.tensor_tensor(dt[t][:].indirect(n1_sb[:]), pb[:, t, :], neg_pa[:, t, :], ADD)
+            for r in range(PACK):
+                nc.scalar.activation(z_bf[r][:, :, t], dt[t][:, r::PACK], COPY, scale=ga_late[:, t : t + 1])
+
+        w3_bf = sb.tile([P, N, PACK], BF16, name="w3_bf", tag="z2_rows_then_ga", align_bytes=64)
+        nc.scalar.copy(
+            w3_bf[:].rearrange("p (c i) j -> p c j i", i=4), w3_raw[:].rearrange("p j (c i) -> p c j i", i=4)
+        )
+        z2_q = quantize("z2", z2_bf[:].rearrange("p c t -> p (c t)"), V)
+        half_old.append(gather_half_old(2, "neg_pa_then_half_old2"))
 
         s_acc = []
         for r in range(PACK):
@@ -183,25 +204,37 @@ def tile_picked_valliftpagex_none_p_kernel(
             acc = bank(r, [P, V])
             product(acc[:], z_q, slice(0, P), z2_q)
             s_acc.append(acc)
+            if r == 0:
+                half_old.append(gather_half_old(3, "z_bf0"))
 
-        z3_bf = [sb.tile([P, OUT_CHUNK, PACK], BF16, name="z3_bf%d" % c, align_bytes=64) for c in range(U // OUT_CHUNK)]
+        z3_bf = [sb.tile([P, width, PACK], BF16, name="z3_bf%d" % c, align_bytes=64) for c, width in enumerate(OUT_CHUNKS)]
         nw = sb.tile([P, PACK, V], F32, name="nw")
-        for t in range(PACK):
-            nc.vector.scalar_tensor_tensor(nw[:, t, :], s_acc[t][:], 0.0625, half_old[:, t, :], MULT, MAX)
-        for t in range(PACK):
-            nc.vector.tensor_copy(page[t][:].indirect(n3_sb[:]), nw[:, t, :])
-            for c in range(U // OUT_CHUNK):
-                nc.scalar.activation(
-                    z3_bf[c][:, :, t], page[t][:, c * OUT_CHUNK : (c + 1) * OUT_CHUNK], COPY, scale=gt_sb[:, t : t + 1]
-                )
 
-        for c in range(U // OUT_CHUNK):
-            z3_q = quantize("z3_%d" % c, z3_bf[c][:].rearrange("p w t -> p (w t)"), OUT_CHUNK)
-            for pair in range(2):
-                acc = bank((PACK + 2 * c + pair) % 8, [P, 2, OUT_CHUNK])
-                for i in range(2):
-                    mt = 2 * pair + i
-                    product(acc[:, i, :], w3_q, slice(mt * P, (mt + 1) * P), z3_q)
-                result = sb.tile([P, 2, OUT_CHUNK], F32, name="result%d_%d" % (c, pair))
-                nc.vector.tensor_tensor(result[:], acc[:], res_sb[c, pair][:], ADD)
-                nc.sync.dma_start(out_rows[:, 2 * pair : 2 * pair + 2, c * OUT_CHUNK : (c + 1) * OUT_CHUNK], result[:])
+        def larger(t):
+            nc.vector.scalar_tensor_tensor(nw[:, t, :], s_acc[t][:], 0.0625, half_old[t][:], MULT, MAX)
+
+        larger(0)
+        for t in range(PACK):
+            if t + 1 < PACK:
+                larger(t + 1)
+            else:
+                w3_q = quantize("w3", w3_bf[:].rearrange("p c j -> p (c j)"), N)
+            nc.vector.tensor_copy(page[t][:].indirect(n3_sb[:]), nw[:, t, :])
+            for c, cols in enumerate(chunks):
+                nc.scalar.activation(z3_bf[c][:, :, t], page[t][:, cols], COPY, scale=gt_sb[:, t : t + 1])
+
+        def quantize_z3(c):
+            grouped = z3_bf[c][:].rearrange("p w t -> p (w t)")
+            return quantize("z3_%d" % c, grouped, OUT_CHUNKS[c], tag="z3_codes%d" % (c % 2))
+
+        z3_q = [quantize_z3(0), quantize_z3(1)]
+        for number, (c, rows, res_piece) in enumerate(pieces):
+            shape = list(res_piece.shape)
+            acc = bank(number, shape)
+            for mt in range(rows.start, rows.stop):
+                product(acc[:, mt - rows.start, :], w3_q, slice(mt * P, (mt + 1) * P), z3_q[c])
+            result = sb.tile(shape, F32, name="result%d" % number)
+            nc.vector.tensor_tensor(result[:], acc[:], res_piece[:], ADD)
+            nc.sync.dma_start(out_rows[:, rows, chunks[c]], result[:])
+            if rows.stop == PACK and c + 2 < len(chunks):
+                z3_q.append(quantize_z3(c + 2))

@@ -21,7 +21,7 @@ P = 128
 PACK = 4
 OUT_CHUNKS = (128, 128, 256, 256, 256)
 BANK = 512
-W1_PARTS = 4
+W1_PARTS = 2
 
 
 def tile_picked_valliftpagex_none_p_kernel(
@@ -85,7 +85,7 @@ def tile_picked_valliftpagex_none_p_kernel(
         nc.sync.dma_start(page[0][:], mem_rows[0])
         n1_sb = load_list(n1, "n1_sb")
         n2_sb = load_list(n2, "n2_sb")
-        w2_raw = sb.tile([P, PACK, H], F32, name="w2_raw")
+        w2_raw = sb.tile([P, PACK, H], F32, name="w2_raw", tag="w2_raw_then_rb", align_bytes=64)
         nc.sync.dma_start(w2_raw[:], w2.rearrange("(p j) c -> p j c", j=PACK))
         gains = []
         for name, src in (("gb_sb", gb), ("ga_sb", ga), ("gt_sb", gt)):
@@ -121,8 +121,7 @@ def tile_picked_valliftpagex_none_p_kernel(
         w1_bf = sb.tile([P, PACK, P, PACK], BF16, name="w1_bf", align_bytes=64)
         part_m = P // W1_PARTS
         for part in range(W1_PARTS):
-            cast = nc.vector.tensor_copy if part == W1_PARTS - 1 else nc.scalar.copy
-            cast(
+            nc.scalar.copy(
                 w1_bf[:, :, part * part_m : (part + 1) * part_m, :].rearrange("p t m j -> p m t j"),
                 w1_raw[part][:].rearrange("p j (m t) -> p m t j", t=PACK),
             )
@@ -145,10 +144,10 @@ def tile_picked_valliftpagex_none_p_kernel(
             nc.scalar.copy(tile[:], acc[:])
             a_sb.append(tile)
 
-        w2_bf = sb.tile([P, PACK, P, PACK], BF16, name="w2_bf", tag="w2_bf_then_rb", align_bytes=64)
+        w2_bf = sb.tile([P, PACK, P, PACK], BF16, name="w2_bf", align_bytes=64)
         nc.scalar.copy(w2_bf[:].rearrange("p t m j -> p m t j"), w2_raw[:].rearrange("p j (m t) -> p m t j", t=PACK))
 
-        neg_pa = sb.tile([P, PACK, W], F32, name="neg_pa", tag="neg_pa_then_half_old2", align_bytes=64)
+        neg_pa = sb.tile([P, PACK, W], F32, name="neg_pa")
         pb = sb.tile([P, PACK, W], F32, name="pb")
         for t in range(PACK):
             nc.vector.tensor_scalar(neg_pa[:, t, :], a_sb[t][:].indirect(n1_sb[:]), -1.0, 0.0, MULT, ADD)
@@ -168,44 +167,48 @@ def tile_picked_valliftpagex_none_p_kernel(
         ga_late = sb.tile([P, PACK], F32, name="ga_late", tag="z2_rows_then_ga", align_bytes=64)
         nc.scalar.copy(ga_late[:], ga_sb[:])
 
-        rb = sb.tile([P, PACK, W], F32, name="rb", tag="w2_bf_then_rb", align_bytes=64)
-        nc.vector.scalar_tensor_tensor(
-            rb[:].rearrange("p t w -> p (t w)"),
-            neg_pa[:].rearrange("p t w -> p (t w)"),
-            -0.5,
-            pb[:].rearrange("p t w -> p (t w)"),
-            MULT,
-            MAX,
-        )
-        dt = [sb.tile([P, S], F32, name="dt%d" % t) for t in range(PACK)]
-        z_bf = [sb.tile([P, P, PACK], BF16, name="z_bf%d" % r, align_bytes=64) for r in range(PACK)]
+        rb = sb.tile([P, PACK * W], F32, name="rb", tag="w2_raw_then_rb", align_bytes=64)
+        for half in range(2):
+            tiles = slice(2 * half, 2 * half + 2)
+            nc.vector.scalar_tensor_tensor(
+                rb[:, 2 * half * W : (2 * half + 2) * W],
+                neg_pa[:, tiles, :].rearrange("p t w -> p (t w)"),
+                -0.5,
+                pb[:, tiles, :].rearrange("p t w -> p (t w)"),
+                MULT,
+                MAX,
+            )
+        dt = [sb.tile([P, S], F32, name="dt%d" % t, align_bytes=64) for t in range(PACK)]
+        z_bf = sb.tile([P, PACK, P, PACK], BF16, name="z_bf", align_bytes=64)
 
         def put_rb(t):
-            nc.vector.tensor_copy(dt[t][:].indirect(n2_sb[:]), rb[:, t, :])
+            nc.vector.tensor_copy(dt[t][:].indirect(n2_sb[:]), rb[:, t * W : (t + 1) * W])
 
         put_rb(0)
         for t in range(PACK):
             if t + 1 < PACK:
                 put_rb(t + 1)
             nc.vector.tensor_tensor(dt[t][:].indirect(n1_sb[:]), pb[:, t, :], neg_pa[:, t, :], ADD)
-            for r in range(PACK):
-                nc.scalar.activation(z_bf[r][:, :, t], dt[t][:, r::PACK], COPY, scale=ga_late[:, t : t + 1])
+            nc.scalar.activation(
+                z_bf[:, :, :, t].rearrange("p r m -> p m r"),
+                dt[t][:].rearrange("p (m r) -> p m r", r=PACK),
+                COPY,
+                scale=ga_late[:, t : t + 1],
+            )
 
         w3_bf = sb.tile([P, N, PACK], BF16, name="w3_bf", tag="z2_rows_then_ga", align_bytes=64)
         nc.scalar.copy(
             w3_bf[:].rearrange("p (c i) j -> p c j i", i=4), w3_raw[:].rearrange("p j (c i) -> p c j i", i=4)
         )
+        half_old.append(gather_half_old(2, "w2_raw_then_rb"))
         z2_q = quantize("z2", z2_bf[:].rearrange("p c t -> p (c t)"), V)
-        half_old.append(gather_half_old(2, "neg_pa_then_half_old2"))
-
+        z_q = quantize("z", z_bf[:].rearrange("p r m t -> p (r m t)"), S)
+        half_old.append(gather_half_old(3, "dt3"))
         s_acc = []
         for r in range(PACK):
-            z_q = quantize("z_cols%d" % r, z_bf[r][:].rearrange("p m t -> p (m t)"), P)
             acc = bank(r, [P, V])
-            product(acc[:], z_q, slice(0, P), z2_q)
+            product(acc[:], z_q, slice(r * P, (r + 1) * P), z2_q)
             s_acc.append(acc)
-            if r == 0:
-                half_old.append(gather_half_old(3, "z_bf0"))
 
         z3_bf = [sb.tile([P, width, PACK], BF16, name="z3_bf%d" % c, align_bytes=64) for c, width in enumerate(OUT_CHUNKS)]
         nw = sb.tile([P, PACK, V], F32, name="nw")

@@ -106,7 +106,7 @@ def tile_picked_valliftpagex_none_p_kernel(
             start = start + width
         pieces = []
         for c, cols in enumerate(chunks):
-            per_bank = BANK // OUT_CHUNKS[c]
+            per_bank = min(2, BANK // OUT_CHUNKS[c]) if c == 0 else BANK // OUT_CHUNKS[c]
             for first in range(0, PACK, per_bank):
                 rows = slice(first, first + per_bank)
                 tile = sb.tile([P, per_bank, OUT_CHUNKS[c]], F32, name="res%d_%d" % (c, first))
@@ -211,20 +211,20 @@ def tile_picked_valliftpagex_none_p_kernel(
             s_acc.append(acc)
 
         z3_bf = [sb.tile([P, width, PACK], BF16, name="z3_bf%d" % c, align_bytes=64) for c, width in enumerate(OUT_CHUNKS)]
-        nw = sb.tile([P, PACK, V], F32, name="nw")
+        nw = [sb.tile([P, V], F32, name="nw%d" % t, align_bytes=64) for t in range(PACK)]
 
         def larger(t):
-            nc.vector.scalar_tensor_tensor(nw[:, t, :], s_acc[t][:], 0.0625, half_old[t][:], MULT, MAX)
+            nc.vector.scalar_tensor_tensor(nw[t][:], s_acc[t][:], 0.0625, half_old[t][:], MULT, MAX)
 
         larger(0)
         for t in range(PACK):
             if t + 1 < PACK:
                 larger(t + 1)
-            else:
-                w3_q = quantize("w3", w3_bf[:].rearrange("p c j -> p (c j)"), N)
-            nc.vector.tensor_copy(page[t][:].indirect(n3_sb[:]), nw[:, t, :])
+            nc.vector.tensor_copy(page[t][:].indirect(n3_sb[:]), nw[t][:])
             for c, cols in enumerate(chunks):
                 nc.scalar.activation(z3_bf[c][:, :, t], page[t][:, cols], COPY, scale=gt_sb[:, t : t + 1])
+
+        w3_q = quantize("w3", w3_bf[:].rearrange("p c j -> p (c j)"), N, tag="nw2")
 
         def quantize_z3(c):
             grouped = z3_bf[c][:].rearrange("p w t -> p (w t)")
@@ -233,7 +233,7 @@ def tile_picked_valliftpagex_none_p_kernel(
         z3_q = [quantize_z3(0), quantize_z3(1)]
         for number, (c, rows, res_piece) in enumerate(pieces):
             shape = list(res_piece.shape)
-            acc = bank(number, shape)
+            acc = bank(number % 8, shape)
             for mt in range(rows.start, rows.stop):
                 product(acc[:, mt - rows.start, :], w3_q, slice(mt * P, (mt + 1) * P), z3_q[c])
             result = sb.tile(shape, F32, name="result%d" % number)

@@ -122,8 +122,8 @@ def tile_picked_valliftpagex_none_p_kernel(
         part_m = P // W1_PARTS
         for part in range(W1_PARTS):
             nc.scalar.copy(
-                w1_bf[:, :, part * part_m : (part + 1) * part_m, :].rearrange("p t m j -> p m t j"),
-                w1_raw[part][:].rearrange("p j (m t) -> p m t j", t=PACK),
+                w1_bf[:, :, part * part_m : (part + 1) * part_m, :].rearrange("p t m j -> p m j t"),
+                w1_raw[part][:].rearrange("p j (m t) -> p m j t", t=PACK),
             )
         w1_q = quantize("w1", w1_bf[:].rearrange("p t m j -> p (t m j)"), H)
         nc.vector.tensor_copy(xa[0][:], xw_all[:].indirect(offs_sb[:]))
@@ -145,7 +145,7 @@ def tile_picked_valliftpagex_none_p_kernel(
             a_sb.append(tile)
 
         w2_bf = sb.tile([P, PACK, P, PACK], BF16, name="w2_bf", align_bytes=64)
-        nc.scalar.copy(w2_bf[:].rearrange("p t m j -> p m t j"), w2_raw[:].rearrange("p j (m t) -> p m t j", t=PACK))
+        nc.scalar.copy(w2_bf[:].rearrange("p t m j -> p m j t"), w2_raw[:].rearrange("p j (m t) -> p m j t", t=PACK))
 
         neg_pa = sb.tile([P, PACK, W], F32, name="neg_pa")
         pb = sb.tile([P, PACK, W], F32, name="pb")

from contextlib import ExitStack

import concourse.mybir as mybir

K, T, S, V, N, H, W, U = 512, 2048, 512, 512, 512, 512, 256, 1024
FLOPS = 2 * 512 * 512 * 512 * 3 + 2 * 512 * 512 * 1024

F32 = mybir.dt.float32
BF16 = mybir.dt.bfloat16
I32 = mybir.dt.int32
U32 = mybir.dt.uint32
U16 = mybir.dt.uint16
U8 = mybir.dt.uint8
FP8X4 = mybir.dt.float8_e4m3fn_x4
MULT = mybir.AluOpType.mult
ADD = mybir.AluOpType.add
MAX = mybir.AluOpType.max
COPY = mybir.ActivationFunctionType.Copy

P = 128
PACK = 4
OUT_CHUNKS = (128, 128, 256, 256, 256)
BANK = 512
W1_PARTS = 2


def tile_picked_valliftpagex_none_p_kernel(
    tc, x_words, x_scales, w1, w2, ga, gb, mem, gt, res, w3, offs, two, n1, n2, n3, out
):
    nc = tc.nc
    with ExitStack() as ctx:
        lists = ctx.enter_context(tc.tile_pool(name="lists", bufs=1))
        sb = ctx.enter_context(tc.tile_pool(name="sb", bufs=1))
        psum = ctx.enter_context(tc.psum_pool(name="psum", bufs=1))

        def load_list(src, name):
            tile = lists.tile(list(src.shape), U16, name=name)
            nc.sync.dma_start(tile[:], src)
            return tile

        def mx_tiles(name, width, tag=None):
            codes = sb.tile([P, width], U32, name=name + "_codes", tag=tag or name + "_codes", align_bytes=64)
            scales = sb.tile([P, width], U8, name=name + "_scales", align_bytes=64)
            return codes, scales

        def quantize(name, grouped, width, tag=None):
            codes, scales = mx_tiles(name, width, tag)
            nc.vector.quantize_mx(out=codes[:].bitcast(FP8X4), scales=scales[:], in_=grouped)
            return codes, scales

        def product(acc, stationary, cols, moving):
            nc.tensor.matmul_mx(
                out=acc,
                lhsT=stationary[0][:, cols].bitcast(FP8X4),
                lhsT_scale=stationary[1][:, cols],
                rhs=moving[0][:].bitcast(FP8X4),
                rhs_scale=moving[1][:],
                start=True,
                stop=True,
            )

        def bank(number, shape):
            return psum.tile(shape, F32, name="bank%d" % number, tag="bank%d" % number)

        offs_sb = load_list(offs, "offs_sb")
        two_sb = load_list(two, "two_sb")
        w1_rows = w1.rearrange("(p j) c -> p j c", j=PACK)
        w1_raw = [sb.tile([P, PACK, H // W1_PARTS], F32, name="w1_raw%d" % part) for part in range(W1_PARTS)]

        def load_w1(part):
            nc.sync.dma_start(w1_raw[part][:], w1_rows[:, :, part * (H // W1_PARTS) : (part + 1) * (H // W1_PARTS)])

        load_w1(0)
        xs_all = sb.tile([P, T], U8, name="xs_all", align_bytes=64)
        nc.vector.memset(xs_all[:].bitcast(I32), 0)
        for q in range(4):
            nc.sync.dma_start(xs_all[32 * q : 32 * q + 4, :].bitcast(I32), x_scales[0, 4 * q : 4 * q + 4, :].bitcast(I32))
        for part in range(1, W1_PARTS):
            load_w1(part)
        xw_all = sb.tile([P, T], U32, name="xw_all", align_bytes=64)
        nc.sync.dma_start(xw_all[:].bitcast(I32), x_words[0].rearrange("p n t -> p (n t)").bitcast(I32))
        n3_sb = load_list(n3, "n3_sb")
        mem_rows = mem.rearrange("(p t) w -> t p w", t=PACK)
        page = [sb.tile([P, U], F32, name="page%d" % t) for t in range(PACK)]
        nc.sync.dma_start(page[0][:], mem_rows[0])
        n1_sb = load_list(n1, "n1_sb")
        n2_sb = load_list(n2, "n2_sb")
        w2_raw = sb.tile([P, PACK, H], F32, name="w2_raw", tag="w2_raw_then_rb", align_bytes=64)
        nc.sync.dma_start(w2_raw[:], w2.rearrange("(p j) c -> p j c", j=PACK))
        gains = []
        for name, src in (("gb_sb", gb), ("ga_sb", ga), ("gt_sb", gt)):
            tile = sb.tile([P, PACK], F32, name=name)
            nc.sync.dma_start(tile[:], src.rearrange("(p t) o -> p (t o)", t=PACK))
            gains.append(tile)
        gb_sb, ga_sb, gt_sb = gains
        for t in range(1, PACK):
            nc.sync.dma_start(page[t][:], mem_rows[t])
        w3_raw = sb.tile([P, PACK, N], F32, name="w3_raw")
        nc.sync.dma_start(w3_raw[:], w3.rearrange("(p j) c -> p j c", j=PACK))
        res_rows = res.rearrange("(mt p) w -> p mt w", p=P)
        out_rows = out.rearrange("(mt p) w -> p mt w", p=P)
        chunks = []
        start = 0
        for width in OUT_CHUNKS:
            chunks.append(slice(start, start + width))
            start = start + width
        pieces = []
        for c, cols in enumerate(chunks):
            per_bank = min(2, BANK // OUT_CHUNKS[c]) if c == 0 else BANK // OUT_CHUNKS[c]
            for first in range(0, PACK, per_bank):
                rows = slice(first, first + per_bank)
                tile = sb.tile([P, per_bank, OUT_CHUNKS[c]], F32, name="res%d_%d" % (c, first))
                nc.sync.dma_start(tile[:], res_rows[:, rows, cols])
                pieces.append((c, rows, tile))

        xa = mx_tiles("xa", S)
        xb = mx_tiles("xb", V)
        nc.vector.tensor_copy(xa[1][:], xs_all[:].indirect(offs_sb[:]))
        nc.vector.tensor_copy(xb[1][:], xs_all[:].indirect(two_sb[:]))

        w1_bf = sb.tile([P, PACK, P, PACK], BF16, name="w1_bf", align_bytes=64)
        part_m = P // W1_PARTS
        for part in range(W1_PARTS):
            nc.scalar.copy(
                w1_bf[:, :, part * part_m : (part + 1) * part_m, :].rearrange("p t m j -> p m j t"),
                w1_raw[part][:].rearrange("p j (m t) -> p m j t", t=PACK),
            )
        w1_q = quantize("w1", w1_bf[:].rearrange("p t m j -> p (t m j)"), H)
        nc.vector.tensor_copy(xa[0][:], xw_all[:].indirect(offs_sb[:]))
        nc.vector.tensor_copy(xb[0][:], xw_all[:].indirect(two_sb[:]))

        def gather_half_old(t, tag):
            tile = sb.tile([P, V], F32, name="half_old%d" % t, tag=tag, align_bytes=64)
            nc.vector.tensor_scalar(tile[:], page[t][:].indirect(n3_sb[:]), 0.5, 0.0, MULT, ADD)
            return tile

        half_old = [gather_half_old(0, "half_old0")]

        a_sb = []
        for t in range(PACK):
            acc = bank(t, [P, S])
            product(acc[:], w1_q, slice(t * P, (t + 1) * P), xa)
            tile = sb.tile([P, S], F32, name="a%d" % t)
            nc.scalar.copy(tile[:], acc[:])
            a_sb.append(tile)

        w2_bf = sb.tile([P, PACK, P, PACK], BF16, name="w2_bf", align_bytes=64)
        nc.scalar.copy(w2_bf[:].rearrange("p t m j -> p m j t"), w2_raw[:].rearrange("p j (m t) -> p m j t", t=PACK))

        neg_pa = sb.tile([P, PACK, W], F32, name="neg_pa")
        pb = sb.tile([P, PACK, W], F32, name="pb")
        for t in range(PACK):
            nc.vector.tensor_scalar(neg_pa[:, t, :], a_sb[t][:].indirect(n1_sb[:]), -1.0, 0.0, MULT, ADD)
            nc.vector.tensor_copy(pb[:, t, :], a_sb[t][:].indirect(n2_sb[:]))

        half_old.append(gather_half_old(1, "half_old1"))
        w2_q = quantize("w2", w2_bf[:].rearrange("p t m j -> p (t m j)"), H)
        z2_rows = sb.tile([P, PACK, V], BF16, name="z2_rows", tag="z2_rows_then_ga", align_bytes=64)
        for t in range(PACK):
            acc = bank(PACK + t, [P, V])
            product(acc[:], w2_q, slice(t * P, (t + 1) * P), xb)
            nc.scalar.activation(z2_rows[:, t, :], acc[:], COPY, scale=gb_sb[:, t : t + 1])
        z2_bf = sb.tile([P, V, PACK], BF16, name="z2_bf", align_bytes=64)
        nc.scalar.copy(
            z2_bf[:].rearrange("p (c i) t -> p c t i", i=4), z2_rows[:].rearrange("p t (c i) -> p c t i", i=4)
        )
        ga_late = sb.tile([P, PACK], F32, name="ga_late", tag="z2_rows_then_ga", align_bytes=64)
        nc.scalar.copy(ga_late[:], ga_sb[:])

        rb = sb.tile([P, PACK * W], F32, name="rb", tag="w2_raw_then_rb", align_bytes=64)
        for half in range(2):
            tiles = slice(2 * half, 2 * half + 2)
            nc.vector.scalar_tensor_tensor(
                rb[:, 2 * half * W : (2 * half + 2) * W],
                neg_pa[:, tiles, :].rearrange("p t w -> p (t w)"),
                -0.5,
                pb[:, tiles, :].rearrange("p t w -> p (t w)"),
                MULT,
                MAX,
            )
        dt = [sb.tile([P, S], F32, name="dt%d" % t, align_bytes=64) for t in range(PACK)]
        z_bf = sb.tile([P, PACK, P, PACK], BF16, name="z_bf", align_bytes=64)

        def put_rb(t):
            nc.vector.tensor_copy(dt[t][:].indirect(n2_sb[:]), rb[:, t * W : (t + 1) * W])

        put_rb(0)
        for t in range(PACK):
            if t + 1 < PACK:
                put_rb(t + 1)
            nc.vector.tensor_tensor(dt[t][:].indirect(n1_sb[:]), pb[:, t, :], neg_pa[:, t, :], ADD)
            nc.scalar.activation(
                z_bf[:, :, :, t].rearrange("p r m -> p m r"),
                dt[t][:].rearrange("p (m r) -> p m r", r=PACK),
                COPY,
                scale=ga_late[:, t : t + 1],
            )

        w3_bf = sb.tile([P, N, PACK], BF16, name="w3_bf", tag="z2_rows_then_ga", align_bytes=64)
        nc.scalar.copy(
            w3_bf[:].rearrange("p (c i) j -> p c j i", i=4), w3_raw[:].rearrange("p j (c i) -> p c j i", i=4)
        )
        half_old.append(gather_half_old(2, "w2_raw_then_rb"))
        z2_q = quantize("z2", z2_bf[:].rearrange("p c t -> p (c t)"), V)
        z_q = quantize("z", z_bf[:].rearrange("p r m t -> p (r m t)"), S)
        half_old.append(gather_half_old(3, "dt3"))
        s_acc = []
        for r in range(PACK):
            acc = bank(r, [P, V])
            product(acc[:], z_q, slice(r * P, (r + 1) * P), z2_q)
            s_acc.append(acc)

        z3_bf = [sb.tile([P, width, PACK], BF16, name="z3_bf%d" % c, align_bytes=64) for c, width in enumerate(OUT_CHUNKS)]
        nw = [sb.tile([P, V], F32, name="nw%d" % t, align_bytes=64) for t in range(PACK)]

        def larger(t):
            nc.vector.scalar_tensor_tensor(nw[t][:], s_acc[t][:], 0.0625, half_old[t][:], MULT, MAX)

        larger(0)
        for t in range(PACK):
            if t + 1 < PACK:
                larger(t + 1)
            nc.vector.tensor_copy(page[t][:].indirect(n3_sb[:]), nw[t][:])
            for c, cols in enumerate(chunks):
                nc.scalar.activation(z3_bf[c][:, :, t], page[t][:, cols], COPY, scale=gt_sb[:, t : t + 1])

        w3_q = quantize("w3", w3_bf[:].rearrange("p c j -> p (c j)"), N, tag="nw2")

        def quantize_z3(c):
            grouped = z3_bf[c][:].rearrange("p w t -> p (w t)")
            return quantize("z3_%d" % c, grouped, OUT_CHUNKS[c], tag="z3_codes%d" % (c % 2))

        z3_q = [quantize_z3(0), quantize_z3(1)]
        for number, (c, rows, res_piece) in enumerate(pieces):
            shape = list(res_piece.shape)
            acc = bank(number % 8, shape)
            for mt in range(rows.start, rows.stop):
                product(acc[:, mt - rows.start, :], w3_q, slice(mt * P, (mt + 1) * P), z3_q[c])
            result = sb.tile(shape, F32, name="result%d" % number)
            nc.vector.tensor_tensor(result[:], acc[:], res_piece[:], ADD)
            nc.sync.dma_start(out_rows[:, rows, chunks[c]], result[:])
            if rows.stop == PACK and c + 2 < len(chunks):
                z3_q.append(quantize_z3(c + 2))
